import numpy as np, ml_dtypes
CORES = [9,25,41,57]
N = 4
import mx_ref
BF = ml_dtypes.bfloat16
def entries(a):
    return np.ascontiguousarray(a.T).reshape(-1)
def table(e):
    return np.ascontiguousarray(np.reshape(e, (-1, 16)).T).astype(np.int32)
def gentries(a):
    return np.ascontiguousarray(a.reshape(8, 16, -1).transpose(0, 2, 1)).reshape(8, -1)
def gtable(e):
    e = np.asarray(e); return np.ascontiguousarray(e.reshape(8, -1, 16).transpose(0, 2, 1)).reshape(128, -1).astype(np.int32)
def cols(t, e):
    v = np.concatenate([t.reshape(128, -1, 4), np.zeros((128, 1, 4), BF)], axis=1)
    return np.ascontiguousarray(v[:, e]).reshape(128, -1)
def gcols(t, e):
    v = np.concatenate([t.reshape(8, 16, -1, 4), np.zeros((8, 16, 1, 4), BF)], axis=2)
    return np.ascontiguousarray(np.stack([v[g][:, e[g]] for g in range(8)])).reshape(128, -1)
def cut(t, i, w=512):
    return t[:, w * i:w * i + w]
def f(rng, *shape):
    return mx_ref.flush((rng.standard_normal(shape, dtype=np.float32) * np.exp2(rng.integers(-2, 3, shape[:-1] + (1,)))).astype(BF))
def wide(rng, *shape, cols=0):
    v = rng.standard_normal(shape, dtype=np.float32) * np.exp2(rng.integers(-12, 13, shape)).astype(np.float32)
    if cols: v *= np.repeat(np.exp2(rng.integers(-cols, cols + 1, shape[:-2] + (1, shape[-1] // 4))) * (rng.random(shape[:-2] + (1, shape[-1] // 4)) > 0.0625), 4, axis=-1).astype(np.float32)
    return mx_ref.flush(v.astype(BF))
T, CAPP, S, O = 512, 128, 512, 3
def lists(rng, kind=""):
    sn = np.full((N, N, CAPP), -1)
    for s in range(N):
        for d in range(N):
            n = CAPP if kind == "foreign" else 0 if kind == "own" else int(rng.integers(0, CAPP + 1))
            if d != s: sn[s, d, rng.permutation(CAPP)[:n]] = rng.integers(0, T, n)
    if kind == "one":
        s, d = rng.permutation(N)[:2]; sn[s, d] = rng.integers(0, T)
    ql = []
    for r in range(N):
        slots = T + np.flatnonzero(sn[:, r].reshape(-1) >= 0)
        if kind == "foreign": e = rng.permutation(np.resize(slots, 4 * S)).reshape(4, S)
        elif kind == "own": e = rng.integers(0, T, (4, S))
        else: e = rng.choice(np.concatenate([np.arange(T), slots]), (4, S))
        if kind == "whole": e = np.repeat(e[:1], 4, axis=0)
        if kind == "one":
            for u in rng.permutation(4)[:int(rng.integers(1, 5))]: e[u] = e[u, 0]
        ql.append(gtable(np.repeat(e, 2, axis=0)))
    return {"sn": np.stack([table(sn[s].reshape(-1)) for s in range(N)]), "ql": np.stack(ql)}
def setup_inputs(rng):
    return {"x": f(rng, N, 128, 4 * T), "w": f(rng, N, 128, O * 512), **lists(rng)}
def setup_inputs_whole(rng):
    return {**setup_inputs(rng), **lists(rng, "whole")}
def setup_inputs_foreign(rng):
    return {**setup_inputs(rng), **lists(rng, "foreign")}
def setup_inputs_own(rng):
    return {**setup_inputs(rng), **lists(rng, "own")}
def setup_inputs_one(rng):
    return {**setup_inputs(rng), **lists(rng, "one")}
def setup_inputs_spread(rng):
    d = setup_inputs(rng); d["x"] = wide(rng, N, 128, 4 * T, cols=8); return d
def check_inputs(d):
    b = []; to = [entries(d["sn"][s]).reshape(N, CAPP) for s in range(N)]
    for r in range(N):
        if to[r].min() < -1 or to[r].max() >= T or (to[r][r] != -1).any(): b.append("sn")
        e = gentries(d["ql"][r]); there = np.concatenate([np.ones(T, bool)] + [to[s][r] >= 0 for s in range(N)])
        if e.min() < 0 or e.max() >= T + N * CAPP or not there[np.clip(e, 0, T + N * CAPP - 1)].all() or (e[0::2] != e[1::2]).any(): b.append("ql")
    return b
def reference(x, w, sn, ql):
    to = [entries(sn[s]).reshape(N, CAPP) for s in range(N)]
    y = np.zeros((N, 128, O * S), np.float32)
    for r in range(N):
        have = np.concatenate([x[r]] + [cols(x[s], to[s][r]) for s in range(N)], axis=1)
        V = mx_ref.quantize(gcols(have, gentries(ql[r])))
        for o in range(O): y[r][:, S * o:S * o + S] = mx_ref.matmul(mx_ref.quantize(np.ascontiguousarray(cut(w[r], o))), V)
    return {"y": y}

@@ -1,0 +1,136 @@
+from concourse.bass import DstId, RemoteDMATransfer
+from concourse.mybir import dt, ActivationFunctionType
+
+N, TC, CAPP, S, O = 4, 512, 128, 512, 3
+X0 = 384
+CH = [(0, 256), (256, 512)]
+
+SCRATCH = {
+    "xt": ("sbuf", [128, 4 * TC], "bfloat16"),
+    "wt": ("sbuf", [128, 512 * O], "bfloat16"),
+    "snt": ("sbuf", [128, N * CAPP // 16], "int32"),
+    "sof": ("sbuf", [128, N * CAPP // 16], "uint16"),
+    "qlt": ("sbuf", [128, S // 16], "int32"),
+    "qof": ("sbuf", [128, S // 16], "uint16"),
+    "qx": ("sbuf", [128, TC], "float8_e4m3fn_x4"),
+    "qxs": ("sbuf", [128, TC], "uint8"),
+    "pc": ("sbuf", [128, (N - 1) * CAPP], "float8_e4m3fn_x4"),
+    "pcs": ("sbuf", [128, (N - 1) * CAPP], "uint8"),
+    "win": ("sbuf", [128, TC + N * CAPP], "float8_e4m3fn_x4"),
+    "wins": ("sbuf", [128, TC + N * CAPP], "uint8"),
+    "qw": ("sbuf", [128, 128 * O], "float8_e4m3fn_x4"),
+    "qws": ("sbuf", [128, 128 * O], "uint8"),
+    "vq": ("sbuf", [128, S], "float8_e4m3fn_x4"),
+    "vqs": ("sbuf", [128, S], "uint8"),
+    "yt": ("sbuf", [128, S * O], "float32"),
+    "ps": ("psum", [128, 512 * len(CH) * O], "float32"),
+}
+SEMAPHORES = (["x0", "x1", "snl", "wl", "qll", "sofd", "qd", "pcsd", "wind", "qwd", "qofd", "acode", "ascale", "sent", "st"]
+              + ["pcd%d" % k for k in range(N - 1)]
+              + ["vqd%d" % h for h in range(len(CH))] + ["vqsd%d" % h for h in range(len(CH))]
+              + ["mm%d" % b for b in range(O * len(CH))] + ["yc%d" % b for b in range(O * len(CH))])
+
+
+def _bits(engines):
+    m = 0
+    for e in engines:
+        m |= 1 << e
+    return m
+
+
+def rank_program(g, core, T, topo):
+    r = T.rank_of(core)
+    if r is None:
+        return
+    sem = T.sem
+    COPY = ActivationFunctionType.Copy
+    dests = [(r + k) % N for k in range(1, N)]
+
+    g.sync.dma_start(T.xt[:, 0:4 * X0], T.x[:, 0:4 * X0]).then_inc(sem.x0, 16)
+    g.sync.dma_start(T.xt[:, 4 * X0:4 * TC], T.x[:, 4 * X0:4 * TC]).then_inc(sem.x1, 16)
+    for k in range(8):
+        g.scalar.dma_start(T.snt[16 * k:16 * k + 16, :], T.sn[:, :]).then_inc(sem.snl, 16)
+    g.sync.wait_ge(sem.x0, 16)
+    g.sync.dma_start(T.wt[:, :], T.w[:, :]).then_inc(sem.wl, 16)
+    g.sync.dma_start(T.qlt[:, :], T.ql[:, :]).then_inc(sem.qll, 16)
+
+    v = g.vector
+    v.wait_ge(sem.x0, 16)
+    v.quantize_mx(T.qx[:, 0:X0], T.qxs[:, 0:X0], T.xt[:, 0:4 * X0]).then_inc(sem.qd, 1)
+    v.wait_ge(sem.snl, 128)
+    v.tensor_copy(T.sof[:, :], T.snt[:, :]).then_inc(sem.sofd, 1)
+    v.wait_ge(sem.x1, 16)
+    v.quantize_mx(T.qx[:, X0:TC], T.qxs[:, X0:TC], T.xt[:, 4 * X0:4 * TC]).then_inc(sem.qd, 1)
+    v.wait_ge(sem.sofd, 1)
+    v.wait_ge(sem.qd, 2)
+    g.scalar.wait_ge(sem.sofd, 1)
+    g.scalar.wait_ge(sem.qd, 2)
+    for k, d in enumerate(dests):
+        a, b, o = CAPP * k, CAPP * k + CAPP, CAPP // 16 * d
+        v.tensor_copy(T.pc[:, a:b].bitcast(dt.uint32),
+                      T.qx[:, 0:TC].bitcast(dt.uint32).indirect(T.sof[:, o:o + CAPP // 16])).then_inc(sem["pcd%d" % k], 1)
+        g.scalar.activation(T.pcs[:, a:b], T.qxs[:, 0:TC].indirect(T.sof[:, o:o + CAPP // 16]), COPY).then_inc(sem.pcsd, 1)
+
+    eng = [topo.engines(core, T.cores[d]) for d in dests]
+    n = len(eng[0])
+    cm = [_bits(eng[0]), _bits(eng[1][:n // 2]), _bits(eng[2][n // 2:])]
+    sm = [_bits(eng[0][:n // 2]), _bits(eng[1][n // 2:3 * n // 4]), _bits(eng[2][3 * n // 4:])]
+    L = TC + CAPP * r
+
+    def codes(k):
+        return T.win[:, L:L + CAPP].bitcast(dt.uint8), T.pc[:, CAPP * k:CAPP * k + CAPP].bitcast(dt.uint8)
+
+    def transfer(k, out, src, m, s):
+        rid, pid, _ = topo.addr(T.cores[dests[k]])
+        return RemoteDMATransfer(dst_ids=[DstId(rid=rid, pnc=pid)], dma_engine_mask=m, remote_sem=s, src=src, dst=out)
+
+    rid, pid, _ = topo.addr(T.cores[dests[0]])
+    g.wait_ge(sem.pcd0, 1)
+    out, src = codes(0)
+    g.remote_dma(out, src, sem.acode, sem.sent, pid, rid, cm[0])
+    g.wait_ge(sem.pcd1, 1)
+    g.wait_ge(sem.pcd2, 1)
+    g.remote_dma_fused([transfer(k, *codes(k), cm[k], sem.acode) for k in (1, 2)], local_sem=sem.sent)
+    g.wait_ge(sem.pcsd, 3)
+    g.remote_dma_fused([transfer(k, T.wins[:, L:L + CAPP], T.pcs[:, CAPP * k:CAPP * k + CAPP], sm[k], sem.ascale)
+                        for k in range(N - 1)], local_sem=sem.sent)
+    g.wait_ge(sem.sent, 3 * n)
+
+    v.quantize_mx(T.win[:, 0:TC], T.wins[:, 0:TC], T.xt[:, 0:4 * TC]).then_inc(sem.wind, 1)
+    v.wait_ge(sem.wl, 16)
+    v.quantize_mx(T.qw[:, 0:128 * O], T.qws[:, 0:128 * O], T.wt[:, 0:512 * O]).then_inc(sem.qwd, 1)
+    v.wait_ge(sem.qll, 16)
+    v.tensor_copy(T.qof[:, :], T.qlt[:, :]).then_inc(sem.qofd, 1)
+
+    v.wait_ge(sem.wind, 1)
+    v.wait_ge(sem.qofd, 1)
+    v.wait_ge(sem.acode, 2 * n)
+    g.scalar.wait_ge(sem.wind, 1)
+    g.scalar.wait_ge(sem.qofd, 1)
+    g.scalar.wait_ge(sem.ascale, n)
+    W = TC + N * CAPP
+    for h, (a, b) in enumerate(CH):
+        off = T.qof[:, a // 16:b // 16]
+        v.tensor_copy(T.vq[:, a:b].bitcast(dt.uint32), T.win[:, 0:W].bitcast(dt.uint32).indirect(off)).then_inc(sem["vqd%d" % h], 1)
+        g.scalar.activation(T.vqs[:, a:b], T.wins[:, 0:W].indirect(off), COPY).then_inc(sem["vqsd%d" % h], 1)
+    g.tensor.wait_ge(sem.qwd, 1)
+    for h, (a, b) in enumerate(CH):
+        g.tensor.wait_ge(sem["vqd%d" % h], 1)
+        g.tensor.wait_ge(sem["vqsd%d" % h], 1)
+        for o in range(O):
+            i = O * h + o
+            g.tensor.matmul_mx(T.ps[:, 512 * i:512 * i + b - a], T.qw[:, 128 * o:128 * o + 128], T.qws[:, 128 * o:128 * o + 128],
+                               T.vq[:, a:b], T.vqs[:, a:b], True, True).then_inc(sem["mm%d" % i], 1)
+    for h, (a, b) in enumerate(CH):
+        for o in range(O):
+            i = O * h + o
+            bank, dst = T.ps[:, 512 * i:512 * i + b - a], T.yt[:, S * o + a:S * o + b]
+            if i % 2 == 0:
+                v.wait_ge(sem["mm%d" % i], 1)
+                v.tensor_copy(dst, bank).then_inc(sem["yc%d" % i], 1)
+            else:
+                g.scalar.wait_ge(sem["mm%d" % i], 1)
+                g.scalar.activation(dst, bank, COPY).then_inc(sem["yc%d" % i], 1)
+            g.sync.wait_ge(sem["yc%d" % i], 1)
+            g.sync.dma_start(T.y[:, S * o + a:S * o + b], dst).then_inc(sem.st, 16)
+    g.sync.wait_ge(sem.st, 16 * O * len(CH))

@@ -2,8 +2,12 @@ from concourse.bass import DstId, RemoteDMATransfer
 from concourse.mybir import dt, ActivationFunctionType
 
 N, TC, CAPP, S, O = 4, 512, 128, 512, 3
-X0 = 384
-CH = [(0, 256), (256, 512)]
+XRUNS = [(0, 352), (352, 512)]
+PIECES = [(0, 128), (128, 384), (384, 512)]
+B = 128
+PRODUCTS = [(0, 1, "s"), (4, 5, "s"), (8, 9, "s"), (5, 6, "s"), (6, 7, "v"), (1, 3, "s"), (3, 4, "v"), (9, 11, "s"), (7, 8, "v"), (11, 12, "v")]
+STORES = [(0, 1), (4, 5), (5, 7), (1, 4), (7, 12)]
+BANKS = 8
 
 SCRATCH = {
     "xt": ("sbuf", [128, 4 * TC], "bfloat16"),
@@ -23,12 +27,13 @@ SCRATCH = {
     "vq": ("sbuf", [128, S], "float8_e4m3fn_x4"),
     "vqs": ("sbuf", [128, S], "uint8"),
     "yt": ("sbuf", [128, S * O], "float32"),
-    "ps": ("psum", [128, 512 * len(CH) * O], "float32"),
+    "ps": ("psum", [128, 512 * BANKS], "float32"),
 }
-SEMAPHORES = (["x0", "x1", "snl", "wl", "qll", "sofd", "qd", "pcsd", "wind", "qwd", "qofd", "acode", "ascale", "sent", "st"]
-              + ["pcd%d" % k for k in range(N - 1)]
-              + ["vqd%d" % h for h in range(len(CH))] + ["vqsd%d" % h for h in range(len(CH))]
-              + ["mm%d" % b for b in range(O * len(CH))] + ["yc%d" % b for b in range(O * len(CH))])
+SEMAPHORES = (["x%d" % k for k in range(len(XRUNS))]
+              + ["snl", "wl", "qll", "sofd", "qd", "wind", "qwd", "qofd", "acode", "ascale", "sent", "st"]
+              + ["pcd0", "pcd1", "pcsd0", "pcsd1"]
+              + ["vqd%d" % p for p in range(len(PIECES))] + ["vqsd%d" % p for p in range(len(PIECES))]
+              + ["mm%d" % i for i in range(len(PRODUCTS))] + ["yc%d" % i for i in range(len(PRODUCTS))])
 
 
 def _bits(engines):
@@ -44,93 +49,93 @@ def rank_program(g, core, T, topo):
         return
     sem = T.sem
     COPY = ActivationFunctionType.Copy
-    dests = [(r + k) % N for k in range(1, N)]
+    dests = [r ^ 1] + [d for d in range(N) if d not in (r, r ^ 1)]
+    v, sc = g.vector, g.scalar
 
-    g.sync.dma_start(T.xt[:, 0:4 * X0], T.x[:, 0:4 * X0]).then_inc(sem.x0, 16)
-    g.sync.dma_start(T.xt[:, 4 * X0:4 * TC], T.x[:, 4 * X0:4 * TC]).then_inc(sem.x1, 16)
-    for k in range(8):
-        g.scalar.dma_start(T.snt[16 * k:16 * k + 16, :], T.sn[:, :]).then_inc(sem.snl, 16)
-    g.sync.wait_ge(sem.x0, 16)
+    for k, q in enumerate((g.sync, sc)):
+        q.dma_start(T.snt[16 * k:16 * k + 16, :], T.sn[:, :]).then_inc(sem.snl, 16)
+    for k, (a, b) in enumerate(XRUNS):
+        g.sync.dma_start(T.xt[:, 4 * a:4 * b], T.x[:, 4 * a:4 * b]).then_inc(sem["x%d" % k], 16)
     g.sync.dma_start(T.wt[:, :], T.w[:, :]).then_inc(sem.wl, 16)
     g.sync.dma_start(T.qlt[:, :], T.ql[:, :]).then_inc(sem.qll, 16)
 
-    v = g.vector
-    v.wait_ge(sem.x0, 16)
-    v.quantize_mx(T.qx[:, 0:X0], T.qxs[:, 0:X0], T.xt[:, 0:4 * X0]).then_inc(sem.qd, 1)
-    v.wait_ge(sem.snl, 128)
-    v.tensor_copy(T.sof[:, :], T.snt[:, :]).then_inc(sem.sofd, 1)
-    v.wait_ge(sem.x1, 16)
-    v.quantize_mx(T.qx[:, X0:TC], T.qxs[:, X0:TC], T.xt[:, 4 * X0:4 * TC]).then_inc(sem.qd, 1)
-    v.wait_ge(sem.sofd, 1)
-    v.wait_ge(sem.qd, 2)
-    g.scalar.wait_ge(sem.sofd, 1)
-    g.scalar.wait_ge(sem.qd, 2)
-    for k, d in enumerate(dests):
-        a, b, o = CAPP * k, CAPP * k + CAPP, CAPP // 16 * d
-        v.tensor_copy(T.pc[:, a:b].bitcast(dt.uint32),
-                      T.qx[:, 0:TC].bitcast(dt.uint32).indirect(T.sof[:, o:o + CAPP // 16])).then_inc(sem["pcd%d" % k], 1)
-        g.scalar.activation(T.pcs[:, a:b], T.qxs[:, 0:TC].indirect(T.sof[:, o:o + CAPP // 16]), COPY).then_inc(sem.pcsd, 1)
+    v.wait_ge(sem.snl, 32)
+    for u in range(4):
+        v.tensor_copy(T.sof[32 * u:32 * u + 32, :], T.snt[0:32, :]).then_inc(sem.sofd, 1)
+    for k, (a, b) in enumerate(XRUNS):
+        v.wait_ge(sem["x%d" % k], 16)
+        v.quantize_mx(T.qx[:, a:b], T.qxs[:, a:b], T.xt[:, 4 * a:4 * b]).then_inc(sem.qd, 1)
+    for q in (v, sc):
+        q.wait_ge(sem.sofd, 4)
+        q.wait_ge(sem.qd, len(XRUNS))
+    for k, (a, b, d) in enumerate([(0, CAPP, dests[0]), (CAPP, 3 * CAPP, dests[1])]):
+        off = T.sof[:, CAPP // 16 * d:CAPP // 16 * d + (b - a) // 16]
+        v.tensor_copy(T.pc[:, a:b].bitcast(dt.uint32), T.qx[:, 0:TC].bitcast(dt.uint32).indirect(off)).then_inc(sem["pcd%d" % k], 1)
+        sc.activation(T.pcs[:, a:b], T.qxs[:, 0:TC].indirect(off), COPY).then_inc(sem["pcsd%d" % k], 1)
 
-    eng = [topo.engines(core, T.cores[d]) for d in dests]
-    n = len(eng[0])
-    cm = [_bits(eng[0]), _bits(eng[1][:n // 2]), _bits(eng[2][n // 2:])]
-    sm = [_bits(eng[0][:n // 2]), _bits(eng[1][n // 2:3 * n // 4]), _bits(eng[2][3 * n // 4:])]
+    eng = topo.engines(core, T.cores[dests[0]])
+    n = len(eng)
+    even, odd = eng[0::2], eng[1::2]
     L = TC + CAPP * r
 
-    def codes(k):
-        return T.win[:, L:L + CAPP].bitcast(dt.uint8), T.pc[:, CAPP * k:CAPP * k + CAPP].bitcast(dt.uint8)
-
-    def transfer(k, out, src, m, s):
+    def transfer(k, codes, engines):
         rid, pid, _ = topo.addr(T.cores[dests[k]])
-        return RemoteDMATransfer(dst_ids=[DstId(rid=rid, pnc=pid)], dma_engine_mask=m, remote_sem=s, src=src, dst=out)
+        a, b = CAPP * k, CAPP * k + CAPP
+        if codes:
+            out, src, s = T.win[:, L:L + CAPP].bitcast(dt.uint8), T.pc[:, a:b].bitcast(dt.uint8), sem.acode
+        else:
+            out, src, s = T.wins[:, L:L + CAPP], T.pcs[:, a:b], sem.ascale
+        return RemoteDMATransfer(dst_ids=[DstId(rid=rid, pnc=pid)], dma_engine_mask=_bits(engines), remote_sem=s, src=src, dst=out)
 
-    rid, pid, _ = topo.addr(T.cores[dests[0]])
     g.wait_ge(sem.pcd0, 1)
-    out, src = codes(0)
-    g.remote_dma(out, src, sem.acode, sem.sent, pid, rid, cm[0])
+    g.remote_dma_fused([transfer(0, True, even)], local_sem=sem.sent)
+    g.wait_ge(sem.pcsd0, 1)
+    g.wait_ge(sem.pcsd1, 1)
+    g.remote_dma_fused([transfer(0, False, even), transfer(1, False, odd[:n // 4]), transfer(2, False, odd[n // 4:])], local_sem=sem.sent)
     g.wait_ge(sem.pcd1, 1)
-    g.wait_ge(sem.pcd2, 1)
-    g.remote_dma_fused([transfer(k, *codes(k), cm[k], sem.acode) for k in (1, 2)], local_sem=sem.sent)
-    g.wait_ge(sem.pcsd, 3)
-    g.remote_dma_fused([transfer(k, T.wins[:, L:L + CAPP], T.pcs[:, CAPP * k:CAPP * k + CAPP], sm[k], sem.ascale)
-                        for k in range(N - 1)], local_sem=sem.sent)
-    g.wait_ge(sem.sent, 3 * n)
+    g.remote_dma_fused([transfer(1, True, even), transfer(2, True, odd)], local_sem=sem.sent)
+    g.wait_ge(sem.sent, 5 * n // 2)
 
     v.quantize_mx(T.win[:, 0:TC], T.wins[:, 0:TC], T.xt[:, 0:4 * TC]).then_inc(sem.wind, 1)
-    v.wait_ge(sem.wl, 16)
-    v.quantize_mx(T.qw[:, 0:128 * O], T.qws[:, 0:128 * O], T.wt[:, 0:512 * O]).then_inc(sem.qwd, 1)
     v.wait_ge(sem.qll, 16)
     v.tensor_copy(T.qof[:, :], T.qlt[:, :]).then_inc(sem.qofd, 1)
+    v.wait_ge(sem.wl, 16)
+    v.quantize_mx(T.qw[:, 0:128 * O], T.qws[:, 0:128 * O], T.wt[:, 0:512 * O]).then_inc(sem.qwd, 1)
 
-    v.wait_ge(sem.wind, 1)
-    v.wait_ge(sem.qofd, 1)
-    v.wait_ge(sem.acode, 2 * n)
-    g.scalar.wait_ge(sem.wind, 1)
-    g.scalar.wait_ge(sem.qofd, 1)
-    g.scalar.wait_ge(sem.ascale, n)
+    for q in (v, sc):
+        q.wait_ge(sem.wind, 1)
+        q.wait_ge(sem.qofd, 1)
+    v.wait_ge(sem.acode, 3 * n // 2)
+    sc.wait_ge(sem.ascale, n)
     W = TC + N * CAPP
-    for h, (a, b) in enumerate(CH):
+    for p, (a, b) in enumerate(PIECES):
         off = T.qof[:, a // 16:b // 16]
-        v.tensor_copy(T.vq[:, a:b].bitcast(dt.uint32), T.win[:, 0:W].bitcast(dt.uint32).indirect(off)).then_inc(sem["vqd%d" % h], 1)
-        g.scalar.activation(T.vqs[:, a:b], T.wins[:, 0:W].indirect(off), COPY).then_inc(sem["vqsd%d" % h], 1)
+        v.tensor_copy(T.vq[:, a:b].bitcast(dt.uint32), T.win[:, 0:W].bitcast(dt.uint32).indirect(off)).then_inc(sem["vqd%d" % p], 1)
+        sc.activation(T.vqs[:, a:b], T.wins[:, 0:W].indirect(off), COPY).then_inc(sem["vqsd%d" % p], 1)
     g.tensor.wait_ge(sem.qwd, 1)
-    for h, (a, b) in enumerate(CH):
-        g.tensor.wait_ge(sem["vqd%d" % h], 1)
-        g.tensor.wait_ge(sem["vqsd%d" % h], 1)
-        for o in range(O):
-            i = O * h + o
-            g.tensor.matmul_mx(T.ps[:, 512 * i:512 * i + b - a], T.qw[:, 128 * o:128 * o + 128], T.qws[:, 128 * o:128 * o + 128],
-                               T.vq[:, a:b], T.vqs[:, a:b], True, True).then_inc(sem["mm%d" % i], 1)
-    for h, (a, b) in enumerate(CH):
-        for o in range(O):
-            i = O * h + o
-            bank, dst = T.ps[:, 512 * i:512 * i + b - a], T.yt[:, S * o + a:S * o + b]
-            if i % 2 == 0:
-                v.wait_ge(sem["mm%d" % i], 1)
-                v.tensor_copy(dst, bank).then_inc(sem["yc%d" % i], 1)
-            else:
-                g.scalar.wait_ge(sem["mm%d" % i], 1)
-                g.scalar.activation(dst, bank, COPY).then_inc(sem["yc%d" % i], 1)
-            g.sync.wait_ge(sem["yc%d" % i], 1)
-            g.sync.dma_start(T.y[:, S * o + a:S * o + b], dst).then_inc(sem.st, 16)
-    g.sync.wait_ge(sem.st, 16 * O * len(CH))
+    seen = []
+    for i, (b0, b1, who) in enumerate(PRODUCTS):
+        o, a = divmod(B * b0, S)
+        b = a + B * (b1 - b0)
+        for p, (c, d) in enumerate(PIECES):
+            if c < b and a < d and p not in seen:
+                seen.append(p)
+                g.tensor.wait_ge(sem["vqsd%d" % p], 1)
+                g.tensor.wait_ge(sem["vqd%d" % p], 1)
+        if i >= BANKS:
+            g.tensor.wait_ge(sem["yc%d" % (i - BANKS)], 1)
+        bank, dst = T.ps[:, 512 * (i % BANKS):512 * (i % BANKS) + b - a], T.yt[:, B * b0:B * b1]
+        g.tensor.matmul_mx(bank, T.qw[:, 128 * o:128 * o + 128], T.qws[:, 128 * o:128 * o + 128],
+                           T.vq[:, a:b], T.vqs[:, a:b], True, True).then_inc(sem["mm%d" % i], 1)
+        if who == "s":
+            sc.wait_ge(sem["mm%d" % i], 1)
+            sc.activation(dst, bank, COPY).then_inc(sem["yc%d" % i], 1)
+        else:
+            v.wait_ge(sem["mm%d" % i], 1)
+            v.tensor_copy(dst, bank).then_inc(sem["yc%d" % i], 1)
+    for a, b in STORES:
+        for i, (b0, b1, who) in enumerate(PRODUCTS):
+            if a <= b0 < b:
+                g.sync.wait_ge(sem["yc%d" % i], 1)
+        g.sync.dma_start(T.y[:, B * a:B * b], T.yt[:, B * a:B * b]).then_inc(sem.st, 16)
+    g.sync.wait_ge(sem.st, 16 * len(STORES))

from concourse.bass import DstId, RemoteDMATransfer
from concourse.mybir import dt, ActivationFunctionType

N, TC, CAPP, S, O = 4, 512, 128, 512, 3
XRUNS = [(0, 352), (352, 512)]
PIECES = [(0, 128), (128, 384), (384, 512)]
B = 128
PRODUCTS = [(0, 1, "s"), (4, 5, "s"), (8, 9, "s"), (5, 6, "s"), (6, 7, "v"), (1, 3, "s"), (3, 4, "v"), (9, 11, "s"), (7, 8, "v"), (11, 12, "v")]
STORES = [(0, 1), (4, 5), (5, 7), (1, 4), (7, 12)]
BANKS = 8

SCRATCH = {
    "xt": ("sbuf", [128, 4 * TC], "bfloat16"),
    "wt": ("sbuf", [128, 512 * O], "bfloat16"),
    "snt": ("sbuf", [128, N * CAPP // 16], "int32"),
    "sof": ("sbuf", [128, N * CAPP // 16], "uint16"),
    "qlt": ("sbuf", [128, S // 16], "int32"),
    "qof": ("sbuf", [128, S // 16], "uint16"),
    "qx": ("sbuf", [128, TC], "float8_e4m3fn_x4"),
    "qxs": ("sbuf", [128, TC], "uint8"),
    "pc": ("sbuf", [128, (N - 1) * CAPP], "float8_e4m3fn_x4"),
    "pcs": ("sbuf", [128, (N - 1) * CAPP], "uint8"),
    "win": ("sbuf", [128, TC + N * CAPP], "float8_e4m3fn_x4"),
    "wins": ("sbuf", [128, TC + N * CAPP], "uint8"),
    "qw": ("sbuf", [128, 128 * O], "float8_e4m3fn_x4"),
    "qws": ("sbuf", [128, 128 * O], "uint8"),
    "vq": ("sbuf", [128, S], "float8_e4m3fn_x4"),
    "vqs": ("sbuf", [128, S], "uint8"),
    "yt": ("sbuf", [128, S * O], "float32"),
    "ps": ("psum", [128, 512 * BANKS], "float32"),
}
SEMAPHORES = (["x%d" % k for k in range(len(XRUNS))]
              + ["snl", "wl", "qll", "sofd", "qd", "wind", "qwd", "qofd", "acode", "ascale", "sent", "st"]
              + ["pcd0", "pcd1", "pcsd0", "pcsd1"]
              + ["vqd%d" % p for p in range(len(PIECES))] + ["vqsd%d" % p for p in range(len(PIECES))]
              + ["mm%d" % i for i in range(len(PRODUCTS))] + ["yc%d" % i for i in range(len(PRODUCTS))])


def _bits(engines):
    m = 0
    for e in engines:
        m |= 1 << e
    return m


def rank_program(g, core, T, topo):
    r = T.rank_of(core)
    if r is None:
        return
    sem = T.sem
    COPY = ActivationFunctionType.Copy
    dests = [r ^ 1] + [d for d in range(N) if d not in (r, r ^ 1)]
    v, sc = g.vector, g.scalar

    for k, q in enumerate((g.sync, sc)):
        q.dma_start(T.snt[16 * k:16 * k + 16, :], T.sn[:, :]).then_inc(sem.snl, 16)
    for k, (a, b) in enumerate(XRUNS):
        g.sync.dma_start(T.xt[:, 4 * a:4 * b], T.x[:, 4 * a:4 * b]).then_inc(sem["x%d" % k], 16)
    g.sync.dma_start(T.wt[:, :], T.w[:, :]).then_inc(sem.wl, 16)
    g.sync.dma_start(T.qlt[:, :], T.ql[:, :]).then_inc(sem.qll, 16)

    v.wait_ge(sem.snl, 32)
    for u in range(4):
        v.tensor_copy(T.sof[32 * u:32 * u + 32, :], T.snt[0:32, :]).then_inc(sem.sofd, 1)
    for k, (a, b) in enumerate(XRUNS):
        v.wait_ge(sem["x%d" % k], 16)
        v.quantize_mx(T.qx[:, a:b], T.qxs[:, a:b], T.xt[:, 4 * a:4 * b]).then_inc(sem.qd, 1)
    for q in (v, sc):
        q.wait_ge(sem.sofd, 4)
        q.wait_ge(sem.qd, len(XRUNS))
    for k, (a, b, d) in enumerate([(0, CAPP, dests[0]), (CAPP, 3 * CAPP, dests[1])]):
        off = T.sof[:, CAPP // 16 * d:CAPP // 16 * d + (b - a) // 16]
        v.tensor_copy(T.pc[:, a:b].bitcast(dt.uint32), T.qx[:, 0:TC].bitcast(dt.uint32).indirect(off)).then_inc(sem["pcd%d" % k], 1)
        sc.activation(T.pcs[:, a:b], T.qxs[:, 0:TC].indirect(off), COPY).then_inc(sem["pcsd%d" % k], 1)

    eng = topo.engines(core, T.cores[dests[0]])
    n = len(eng)
    even, odd = eng[0::2], eng[1::2]
    L = TC + CAPP * r

    def transfer(k, codes, engines):
        rid, pid, _ = topo.addr(T.cores[dests[k]])
        a, b = CAPP * k, CAPP * k + CAPP
        if codes:
            out, src, s = T.win[:, L:L + CAPP].bitcast(dt.uint8), T.pc[:, a:b].bitcast(dt.uint8), sem.acode
        else:
            out, src, s = T.wins[:, L:L + CAPP], T.pcs[:, a:b], sem.ascale
        return RemoteDMATransfer(dst_ids=[DstId(rid=rid, pnc=pid)], dma_engine_mask=_bits(engines), remote_sem=s, src=src, dst=out)

    g.wait_ge(sem.pcd0, 1)
    g.remote_dma_fused([transfer(0, True, even)], local_sem=sem.sent)
    g.wait_ge(sem.pcsd0, 1)
    g.wait_ge(sem.pcsd1, 1)
    g.remote_dma_fused([transfer(0, False, even), transfer(1, False, odd[:n // 4]), transfer(2, False, odd[n // 4:])], local_sem=sem.sent)
    g.wait_ge(sem.pcd1, 1)
    g.remote_dma_fused([transfer(1, True, even), transfer(2, True, odd)], local_sem=sem.sent)
    g.wait_ge(sem.sent, 5 * n // 2)

    v.quantize_mx(T.win[:, 0:TC], T.wins[:, 0:TC], T.xt[:, 0:4 * TC]).then_inc(sem.wind, 1)
    v.wait_ge(sem.qll, 16)
    v.tensor_copy(T.qof[:, :], T.qlt[:, :]).then_inc(sem.qofd, 1)
    v.wait_ge(sem.wl, 16)
    v.quantize_mx(T.qw[:, 0:128 * O], T.qws[:, 0:128 * O], T.wt[:, 0:512 * O]).then_inc(sem.qwd, 1)

    for q in (v, sc):
        q.wait_ge(sem.wind, 1)
        q.wait_ge(sem.qofd, 1)
    v.wait_ge(sem.acode, 3 * n // 2)
    sc.wait_ge(sem.ascale, n)
    W = TC + N * CAPP
    for p, (a, b) in enumerate(PIECES):
        off = T.qof[:, a // 16:b // 16]
        v.tensor_copy(T.vq[:, a:b].bitcast(dt.uint32), T.win[:, 0:W].bitcast(dt.uint32).indirect(off)).then_inc(sem["vqd%d" % p], 1)
        sc.activation(T.vqs[:, a:b], T.wins[:, 0:W].indirect(off), COPY).then_inc(sem["vqsd%d" % p], 1)
    g.tensor.wait_ge(sem.qwd, 1)
    seen = []
    for i, (b0, b1, who) in enumerate(PRODUCTS):
        o, a = divmod(B * b0, S)
        b = a + B * (b1 - b0)
        for p, (c, d) in enumerate(PIECES):
            if c < b and a < d and p not in seen:
                seen.append(p)
                g.tensor.wait_ge(sem["vqsd%d" % p], 1)
                g.tensor.wait_ge(sem["vqd%d" % p], 1)
        if i >= BANKS:
            g.tensor.wait_ge(sem["yc%d" % (i - BANKS)], 1)
        bank, dst = T.ps[:, 512 * (i % BANKS):512 * (i % BANKS) + b - a], T.yt[:, B * b0:B * b1]
        g.tensor.matmul_mx(bank, T.qw[:, 128 * o:128 * o + 128], T.qws[:, 128 * o:128 * o + 128],
                           T.vq[:, a:b], T.vqs[:, a:b], True, True).then_inc(sem["mm%d" % i], 1)
        if who == "s":
            sc.wait_ge(sem["mm%d" % i], 1)
            sc.activation(dst, bank, COPY).then_inc(sem["yc%d" % i], 1)
        else:
            v.wait_ge(sem["mm%d" % i], 1)
            v.tensor_copy(dst, bank).then_inc(sem["yc%d" % i], 1)
    for a, b in STORES:
        for i, (b0, b1, who) in enumerate(PRODUCTS):
            if a <= b0 < b:
                g.sync.wait_ge(sem["yc%d" % i], 1)
        g.sync.dma_start(T.y[:, B * a:B * b], T.yt[:, B * a:B * b]).then_inc(sem.st, 16)
    g.sync.wait_ge(sem.st, 16 * len(STORES))
